import numpy as np
import ml_dtypes


def mxq(x, axis, fmt="e4m3"):
    dtype, down = {"e4m3": (ml_dtypes.float8_e4m3fn, 7), "e5m2": (ml_dtypes.float8_e5m2, 14)}[fmt]
    v = np.moveaxis(np.asarray(x, np.float32).astype(ml_dtypes.bfloat16).astype(np.float64), axis, -1)
    blocks = v.reshape(v.shape[:-1] + (-1, 32))
    amax = np.abs(blocks).max(-1, keepdims=True)
    byte = np.maximum(np.where(amax > 0, np.frexp(amax)[1] - 1 + 127, 0) - down, 1)
    scale = np.exp2(byte - 127.0)
    codes = (blocks / scale).astype(np.float32).astype(dtype).astype(np.float64)
    return np.moveaxis((codes * scale).reshape(v.shape), -1, axis)


WIDE = False


def mx_kscale(k):
    if not WIDE:
        return np.ones(k)
    levels = np.array([30, -30])
    if k % 512:
        return np.exp2(np.random.permutation(np.resize(levels, k // 32))).repeat(32)
    a = np.empty((k // 512, 16))
    for p in range(k // 512):
        a[p, :8] = np.random.permutation(np.resize(levels, 8))
        for g in range(8):
            far = levels[np.abs(levels - a[p, g]) >= 10]
            a[p, g + 8] = far[np.random.randint(len(far))]
    return np.exp2(a.ravel()).repeat(32)


def f64(x):
    return np.asarray(x).astype(np.float64)


def striped(idx):
    return np.tile(np.asarray(idx).reshape(-1, 16).T, (8, 1)).astype(np.uint16)


def unstriped(offs):
    return offs[:16].T.reshape(-1).astype(np.int64)


E2M1 = np.array([0.0, 0.5, 1.0, 1.5, 2.0, 3.0, 4.0, 6.0, -0.0, -0.5, -1.0, -1.5, -2.0, -3.0, -4.0, -6.0])


def pack_weight(w, fmt):
    k, n = w.shape
    w = f64(np.asarray(w, np.float32).astype(ml_dtypes.bfloat16)).reshape(k // 32, 32, n)
    amax = np.abs(w).max(1)
    if fmt in ("e4m3", "e5m2"):
        byte = np.frexp(amax)[1] - 1 + 127 - (7 if fmt == "e4m3" else 14)
    else:
        mant, ex = np.frexp(amax / 6.0)
        byte = np.where(mant > 0.5, ex, ex - 1) + 127
    byte = np.clip(np.where(amax > 0, byte, 1), 1, 254)
    scaled = (w * np.exp2(127.0 - byte)[:, None, :]).reshape(k, n).astype(np.float32)
    by_word = np.ascontiguousarray(scaled.reshape(k // 512, 128, 4, n).transpose(0, 1, 3, 2))
    if fmt in ("e4m3", "e5m2"):
        words = by_word.astype(ml_dtypes.float8_e4m3fn if fmt == "e4m3" else ml_dtypes.float8_e5m2).view(np.uint8)
    else:
        c = by_word.astype(ml_dtypes.float4_e2m1fn).view(np.uint8) & 0xF
        words = (c[..., 0::2] | (c[..., 1::2] << 4)).reshape(k // 512, 128, 2 * n)
    return np.ascontiguousarray(words), np.ascontiguousarray(byte.astype(np.uint8).reshape(k // 512, 16, n))


def unpack_weight(words, scales, fmt):
    g, _, n = scales.shape
    words = np.ascontiguousarray(words).reshape(g, 128, n, -1)
    if fmt in ("e4m3", "e5m2"):
        vals = words.view(ml_dtypes.float8_e4m3fn if fmt == "e4m3" else ml_dtypes.float8_e5m2).astype(np.float64)
    else:
        nib = np.empty((g, 128, n, 4), np.uint8)
        nib[..., 0::2] = words & 0xF
        nib[..., 1::2] = words >> 4
        vals = E2M1[nib]
    vals = vals * np.repeat(np.exp2(scales.astype(np.float64) - 127.0), 8, axis=1)[..., None]
    return vals.transpose(0, 1, 3, 2).reshape(g * 512, n)


def e4m3fn_bytes(y):
    return np.clip(np.asarray(y, np.float64), -448.0, 448.0).astype(np.float32).astype(ml_dtypes.float8_e4m3fn).view(np.uint8)


def e4m3fn_values(b):
    return np.asarray(b, np.uint8).view(ml_dtypes.float8_e4m3fn).astype(np.float64)


def sgn(shape):
    return np.random.uniform(0.5, 2.0, shape) * np.where(np.random.standard_normal(shape) < 0, -1.0, 1.0)


K, T, J, R, V, N, E = 512, 1024, 256, 512, 1024, 256, 512


def setup_inputs():
    n = np.random.standard_normal
    idx = np.random.permutation(T)[:J]
    idx2 = np.random.permutation(V)[:J]
    idx3 = np.random.permutation(V)[:J]
    idx4 = np.random.permutation(V)[:J]
    idx5 = np.random.permutation(E)[:J]
    fk = mx_kscale(K)
    fr = mx_kscale(R)
    xtp = pack_weight(n((K, T)) / fk[:, None], "e4m3")
    wp = pack_weight(n((K, R)) * 1 / np.sqrt(K) * fk[:, None], "e2m1")
    wbp = pack_weight(n((R, N)) * 1 / np.sqrt(R) / fr[:, None], "e5m2")
    return {
        "xt_words": xtp[0],
        "xt_scales": xtp[1],
        "w_words": wp[0],
        "w_scales": wp[1],
        "ca": e4m3fn_bytes(60.0 * n((R, V))),
        "st": (np.random.uniform(0.004, 0.012, (R, 1)) * fr[:, None]).astype(np.float32),
        "wb_words": wbp[0],
        "wb_scales": wbp[1],
        "so": (sgn((N, 1))).astype(np.float32),
        "offs": striped(idx),
        "offs2": striped(idx2),
        "offs3": striped(idx3),
        "offs4": striped(idx4),
        "offs5": striped(idx5),
    }


def reference(xt_words, xt_scales, w_words, w_scales, ca, st, wb_words, wb_scales, so, offs, offs2, offs3, offs4, offs5):
    idx = unstriped(offs)
    idx2 = unstriped(offs2)
    idx3 = unstriped(offs3)
    idx4 = unstriped(offs4)
    idx5 = unstriped(offs5)
    xtu = unpack_weight(xt_words, xt_scales, "e4m3")
    wu = unpack_weight(w_words, w_scales, "e2m1")
    wbu = unpack_weight(wb_words, wb_scales, "e5m2")
    xtidxg = xtu[:, idx]
    a = wu.T @ xtidxg
    m1 = np.maximum(np.minimum(e4m3fn_values(ca)[:, idx2], e4m3fn_values(ca)[:, idx3]), np.minimum(np.maximum(e4m3fn_values(ca)[:, idx2], e4m3fn_values(ca)[:, idx3]), e4m3fn_values(ca)[:, idx4]))
    g1 = m1 * f64(st)
    hid = a * g1
    hidq = mxq(hid, 0, "e4m3")
    p = wbu.T @ hidq
    y = np.zeros((N, E))
    y[:, idx5] = p * f64(so)
    return y

@@ -1,0 +1,159 @@
+from contextlib import ExitStack
+
+import concourse.mybir as mybir
+
+K, T, J, R, V, N, E = 512, 1024, 256, 512, 1024, 256, 512
+FLOPS = 2 * K * R * J + 2 * R * N * J
+
+F32 = mybir.dt.float32
+BF16 = mybir.dt.bfloat16
+I32 = mybir.dt.int32
+U32 = mybir.dt.uint32
+U16 = mybir.dt.uint16
+U8 = mybir.dt.uint8
+FP8 = mybir.dt.float8_e4m3fn
+E4M3X4 = mybir.dt.float8_e4m3fn_x4
+E5M2X4 = mybir.dt.float8_e5m2_x4
+E2M1X4 = mybir.dt.float4_e2m1fn_x4
+ALU = mybir.AluOpType
+COPY = mybir.ActivationFunctionType.Copy
+
+P = 128
+PACK = 4
+VOTES = 3
+HALF = J // 2
+LINE = 4
+
+
+def load_scale_rows(nc, plane, rows):
+    for q in range(4):
+        nc.sync.dma_start(plane[32 * q : 32 * q + 4, :].bitcast(I32), rows[4 * q : 4 * q + 4, :].bitcast(I32))
+
+
+def tile_list_majority_kernel(tc, xt_words, xt_scales, w_words, w_scales, ca, st, wb_words, wb_scales, so,
+                                 offs, offs2, offs3, offs4, offs5, out):
+    nc = tc.nc
+    with ExitStack() as ctx:
+        sb = ctx.enter_context(tc.tile_pool(name="sb", bufs=1))
+        ps = ctx.enter_context(tc.psum_pool(name="ps", bufs=1))
+
+        token_list = sb.tile([P, J // 16], U16, name="token_list")
+        vote_lists = [sb.tile([P, J // 16], U16, name="vote_list%d" % v) for v in range(VOTES)]
+        page_list = sb.tile([P, J // 16], U16, name="page_list")
+        store = [sb.tile([P, V], U8, name="store%d" % t) for t in range(PACK)]
+        step = sb.tile([P, PACK], F32, name="step")
+        out_weight = sb.tile([P, N // P], F32, name="out_weight")
+        xt_codes = sb.tile([P, T], U32, name="xt_codes")
+        xt_plane = sb.tile([P, T], U8, name="xt_plane", tag="plane_then_lower")
+        w_codes = sb.tile([P, R], U16, name="w_codes")
+        w_plane = sb.tile([P, R], U8, name="w_plane")
+        wb_codes = sb.tile([P, N], U32, name="wb_codes", align_bytes=64)
+        wb_plane = sb.tile([P, N], U8, name="wb_plane", align_bytes=64)
+        pages = [sb.tile([P, E], F32, name="page%d" % c) for c in range(N // P)]
+
+        for plane in (w_plane, xt_plane, wb_plane):
+            nc.vector.memset(plane[:].bitcast(I32), 0)
+        for page in pages:
+            nc.vector.memset(page[:], 0.0)
+
+        ca_rows = ca.rearrange("(p t) v -> t p v", t=PACK)
+        nc.sync.dma_start(store[0][:], ca_rows[0])
+        for tile, src in zip(vote_lists, (offs2, offs3, offs4)):
+            nc.sync.dma_start(tile[:], src)
+        nc.sync.dma_start(step[:], st.rearrange("(p t) o -> p (t o)", t=PACK))
+        for t in range(1, PACK):
+            nc.sync.dma_start(store[t][:], ca_rows[t])
+        nc.sync.dma_start(w_codes[:].bitcast(I32), w_words[0].bitcast(I32))
+        load_scale_rows(nc, w_plane, w_scales[0])
+        nc.sync.dma_start(xt_codes[:].bitcast(I32), xt_words[0].rearrange("p c b -> p (c b)").bitcast(I32))
+        nc.sync.dma_start(token_list[:], offs)
+        load_scale_rows(nc, xt_plane, xt_scales[0])
+        nc.sync.dma_start(wb_codes[:].bitcast(I32), wb_words[0].rearrange("p c b -> p (c b)").bitcast(I32))
+        load_scale_rows(nc, wb_plane, wb_scales[0])
+        nc.sync.dma_start(page_list[:], offs5)
+        with nc.allow_non_contiguous_dma(reason="one weight a partition"):
+            nc.sync.dma_start(out_weight[:], so.rearrange("(c p) o -> p (c o)", p=P))
+
+        votes = sb.tile([P, PACK, VOTES, J], F32, name="votes")
+        for t in range(PACK):
+            picked = sb.tile([P, VOTES, J], U8, name="picked%d" % t)
+            for v in range(VOTES):
+                nc.vector.tensor_copy(picked[:, v, :], store[t][:].indirect(vote_lists[v][:]))
+            nc.scalar.activation(
+                votes[:, t, :, :].rearrange("p v j -> p (v j)"),
+                picked[:].rearrange("p v j -> p (v j)").bitcast(FP8),
+                COPY,
+                scale=step[:, t : t + 1],
+            )
+
+        w_dealt = sb.tile([P, PACK, P], U16, name="w_dealt", align_bytes=64)
+        w_dealt_plane = sb.tile([P, PACK, P], U8, name="w_dealt_plane", align_bytes=64)
+        nc.scalar.copy(w_dealt[:], w_codes[:].rearrange("p (m t) -> p t m", t=PACK))
+        nc.vector.tensor_copy(w_dealt_plane[:], w_plane[:].rearrange("p (m t) -> p t m", t=PACK))
+
+        x_codes = sb.tile([P, J], U32, name="x_codes", align_bytes=64)
+        x_plane = sb.tile([P, J], U8, name="x_plane", align_bytes=64)
+        nc.vector.tensor_copy(x_codes[:], xt_codes[:].indirect(token_list[:]))
+        nc.vector.tensor_copy(x_plane[:], xt_plane[:].indirect(token_list[:]))
+
+        bounds = sb.tile([P, J // HALF, 2, PACK, HALF], F32, name="bounds", tag="plane_then_lower")
+        for h in range(J // HALF):
+            slots = slice(h * HALF, (h + 1) * HALF)
+            a = ps.tile([P, PACK, HALF], F32, name="a%d" % h)
+            for t in range(PACK):
+                nc.tensor.matmul_mx(
+                    a[:, t, :],
+                    lhsT=w_dealt[:, t, :].bitcast(E2M1X4),
+                    lhsT_scale=w_dealt_plane[:, t, :],
+                    rhs=x_codes[:, slots].bitcast(E4M3X4),
+                    rhs_scale=x_plane[:, slots],
+                    start=True,
+                    stop=True,
+                )
+
+            upper = bounds[:, h, 0, :, :]
+            lower = bounds[:, h, 1, :, :]
+            capped = sb.tile([P, PACK, HALF], F32, name="capped%d" % h)
+            gate = sb.tile([P, PACK, HALF], F32, name="gate%d" % h)
+            nc.vector.tensor_tensor(upper, votes[:, :, 0, slots], votes[:, :, 1, slots], ALU.max)
+            nc.vector.tensor_tensor(lower, votes[:, :, 0, slots], votes[:, :, 1, slots], ALU.min)
+            nc.vector.tensor_tensor(capped[:], upper, votes[:, :, 2, slots], ALU.min)
+            nc.vector.tensor_tensor(gate[:], lower, capped[:], ALU.max)
+
+            hid = sb.tile([P, HALF, PACK], BF16, name="hid%d" % h, align_bytes=64)
+            nc.vector.tensor_tensor(
+                hid[:].rearrange("p (c i) t -> p c t i", i=LINE),
+                gate[:].rearrange("p t (c i) -> p c t i", i=LINE),
+                a[:].rearrange("p t (c i) -> p c t i", i=LINE),
+                ALU.mult,
+            )
+            hid_codes = sb.tile([P, HALF], U32, name="hid_codes%d" % h, align_bytes=64)
+            hid_plane = sb.tile([P, HALF], U8, name="hid_plane%d" % h, align_bytes=64)
+            nc.vector.quantize_mx(hid_codes[:].bitcast(E4M3X4), hid_plane[:], hid[:].rearrange("p j t -> p (j t)"))
+
+            for c in range(N // P):
+                features = slice(c * P, (c + 1) * P)
+                prod = ps.tile([P, HALF], F32, name="prod%d_%d" % (h, c))
+                nc.tensor.matmul_mx(
+                    prod[:],
+                    lhsT=wb_codes[:, features].bitcast(E5M2X4),
+                    lhsT_scale=wb_plane[:, features],
+                    rhs=hid_codes[:].bitcast(E4M3X4),
+                    rhs_scale=hid_plane[:],
+                    start=True,
+                    stop=True,
+                )
+                rows = sb.tile([P, HALF], F32, name="rows%d_%d" % (h, c))
+                if h == 0:
+                    nc.scalar.copy(rows[:], prod[:])
+                else:
+                    nc.vector.tensor_copy(rows[:], prod[:])
+                nc.scalar.activation(
+                    pages[c][:].indirect(page_list[:, h * HALF // 16 : (h + 1) * HALF // 16]),
+                    rows[:],
+                    COPY,
+                    scale=out_weight[:, c : c + 1],
+                )
+
+        for c in range(N // P):
+            nc.sync.dma_start(out[c * P : (c + 1) * P, :], pages[c][:])

@@ -17,12 +17,15 @@ E5M2X4 = mybir.dt.float8_e5m2_x4
 E2M1X4 = mybir.dt.float4_e2m1fn_x4
 ALU = mybir.AluOpType
 COPY = mybir.ActivationFunctionType.Copy
+RELU = mybir.ActivationFunctionType.Relu
 
 P = 128
 PACK = 4
 VOTES = 3
 HALF = J // 2
 LINE = 4
+EARLY = 2
+CHUNKS = ((0, 128), (128, 64), (192, 64))
 
 
 def load_scale_rows(nc, plane, rows):
@@ -44,7 +47,7 @@ def tile_list_majority_kernel(tc, xt_words, xt_scales, w_words, w_scales, ca, st
         step = sb.tile([P, PACK], F32, name="step")
         out_weight = sb.tile([P, N // P], F32, name="out_weight")
         xt_codes = sb.tile([P, T], U32, name="xt_codes")
-        xt_plane = sb.tile([P, T], U8, name="xt_plane", tag="plane_then_lower")
+        xt_plane = sb.tile([P, T], U8, name="xt_plane")
         w_codes = sb.tile([P, R], U16, name="w_codes")
         w_plane = sb.tile([P, R], U8, name="w_plane")
         wb_codes = sb.tile([P, N], U32, name="wb_codes", align_bytes=64)
@@ -58,45 +61,71 @@ def tile_list_majority_kernel(tc, xt_words, xt_scales, w_words, w_scales, ca, st
 
         ca_rows = ca.rearrange("(p t) v -> t p v", t=PACK)
         nc.sync.dma_start(store[0][:], ca_rows[0])
-        for tile, src in zip(vote_lists, (offs2, offs3, offs4)):
+        for tile, src in zip(vote_lists, (offs2, offs3)):
             nc.sync.dma_start(tile[:], src)
-        nc.sync.dma_start(step[:], st.rearrange("(p t) o -> p (t o)", t=PACK))
-        for t in range(1, PACK):
-            nc.sync.dma_start(store[t][:], ca_rows[t])
-        nc.sync.dma_start(w_codes[:].bitcast(I32), w_words[0].bitcast(I32))
+        nc.sync.dma_start(store[1][:], ca_rows[1])
         load_scale_rows(nc, w_plane, w_scales[0])
+        nc.sync.dma_start(step[:], st.rearrange("(p t) o -> p (t o)", t=PACK))
+        for t in range(2, PACK):
+            nc.sync.dma_start(store[t][:], ca_rows[t])
         nc.sync.dma_start(xt_codes[:].bitcast(I32), xt_words[0].rearrange("p c b -> p (c b)").bitcast(I32))
         nc.sync.dma_start(token_list[:], offs)
         load_scale_rows(nc, xt_plane, xt_scales[0])
+        nc.sync.dma_start(vote_lists[2][:], offs4)
+        nc.sync.dma_start(w_codes[:].bitcast(I32), w_words[0].bitcast(I32))
         nc.sync.dma_start(wb_codes[:].bitcast(I32), wb_words[0].rearrange("p c b -> p (c b)").bitcast(I32))
         load_scale_rows(nc, wb_plane, wb_scales[0])
         nc.sync.dma_start(page_list[:], offs5)
         with nc.allow_non_contiguous_dma(reason="one weight a partition"):
             nc.sync.dma_start(out_weight[:], so.rearrange("(c p) o -> p (c o)", p=P))
 
-        votes = sb.tile([P, PACK, VOTES, J], F32, name="votes")
-        for t in range(PACK):
-            picked = sb.tile([P, VOTES, J], U8, name="picked%d" % t)
-            for v in range(VOTES):
-                nc.vector.tensor_copy(picked[:, v, :], store[t][:].indirect(vote_lists[v][:]))
-            nc.scalar.activation(
-                votes[:, t, :, :].rearrange("p v j -> p (v j)"),
-                picked[:].rearrange("p v j -> p (v j)").bitcast(FP8),
-                COPY,
-                scale=step[:, t : t + 1],
-            )
-
-        w_dealt = sb.tile([P, PACK, P], U16, name="w_dealt", align_bytes=64)
         w_dealt_plane = sb.tile([P, PACK, P], U8, name="w_dealt_plane", align_bytes=64)
-        nc.scalar.copy(w_dealt[:], w_codes[:].rearrange("p (m t) -> p t m", t=PACK))
-        nc.vector.tensor_copy(w_dealt_plane[:], w_plane[:].rearrange("p (m t) -> p t m", t=PACK))
+
+        nc.gpsimd.tensor_copy(w_dealt_plane[:], w_plane[:].rearrange("p (m t) -> p t m", t=PACK))
+
+        bounds = sb.tile([P, 2, PACK, J], F32, name="bounds")
+        picked_pairs = []
+        for t in range(PACK):
+            picked = sb.tile([P, 2, J], U8, name="picked_pair%d" % t)
+            for v in range(2):
+                nc.vector.tensor_copy(picked[:, v, :], store[t][:].indirect(vote_lists[v][:]))
+            picked_pairs.append(picked[:].rearrange("p v j -> p (v j)").bitcast(FP8))
+            if t < EARLY:
+                pair = sb.tile([P, 2, J], F32, name="pair%d" % t)
+                gap = sb.tile([P, J], F32, name="gap%d" % t, tag="gap%d" % t, align_bytes=64)
+                excess = sb.tile([P, J], F32, name="excess%d" % t)
+                nc.scalar.activation(
+                    pair[:].rearrange("p v j -> p (v j)"), picked_pairs[t], COPY, scale=step[:, t : t + 1]
+                )
+                nc.gpsimd.tensor_tensor(gap[:], pair[:, 0, :], pair[:, 1, :], ALU.subtract)
+                nc.scalar.activation(excess[:], gap[:], RELU)
+                nc.gpsimd.tensor_tensor(bounds[:, 0, t, :], pair[:, 1, :], excess[:], ALU.add)
+                nc.gpsimd.tensor_tensor(bounds[:, 1, t, :], pair[:, 0, :], excess[:], ALU.subtract)
 
         x_codes = sb.tile([P, J], U32, name="x_codes", align_bytes=64)
         x_plane = sb.tile([P, J], U8, name="x_plane", align_bytes=64)
         nc.vector.tensor_copy(x_codes[:], xt_codes[:].indirect(token_list[:]))
         nc.vector.tensor_copy(x_plane[:], xt_plane[:].indirect(token_list[:]))
 
-        bounds = sb.tile([P, J // HALF, 2, PACK, HALF], F32, name="bounds", tag="plane_then_lower")
+        rest = sb.tile([P, PACK + 2 * (PACK - EARLY), J], F32, name="rest", tag="gap%d" % (EARLY - 1), align_bytes=64)
+        thirds = rest[:, :PACK, :]
+        late_pairs = rest[:, PACK:, :].rearrange("p (t v) j -> p t v j", v=2)
+        for t in range(EARLY, PACK):
+            nc.scalar.activation(
+                late_pairs[:, t - EARLY, :, :].rearrange("p v j -> p (v j)"),
+                picked_pairs[t],
+                COPY,
+                scale=step[:, t : t + 1],
+            )
+        for t in range(PACK):
+            picked = sb.tile([P, J], U8, name="picked_third%d" % t)
+            nc.vector.tensor_copy(picked[:], store[t][:].indirect(vote_lists[2][:]))
+            nc.scalar.activation(thirds[:, t, :], picked[:].bitcast(FP8), COPY, scale=step[:, t : t + 1])
+
+        w_dealt = sb.tile([P, PACK, P], U16, name="w_dealt", tag="gap0", align_bytes=64)
+        nc.scalar.copy(w_dealt[:], w_codes[:].rearrange("p (m t) -> p t m", t=PACK))
+
+        banks = []
         for h in range(J // HALF):
             slots = slice(h * HALF, (h + 1) * HALF)
             a = ps.tile([P, PACK, HALF], F32, name="a%d" % h)
@@ -110,50 +139,69 @@ def tile_list_majority_kernel(tc, xt_words, xt_scales, w_words, w_scales, ca, st
                     start=True,
                     stop=True,
                 )
+            banks.append(a)
 
-            upper = bounds[:, h, 0, :, :]
-            lower = bounds[:, h, 1, :, :]
-            capped = sb.tile([P, PACK, HALF], F32, name="capped%d" % h)
-            gate = sb.tile([P, PACK, HALF], F32, name="gate%d" % h)
-            nc.vector.tensor_tensor(upper, votes[:, :, 0, slots], votes[:, :, 1, slots], ALU.max)
-            nc.vector.tensor_tensor(lower, votes[:, :, 0, slots], votes[:, :, 1, slots], ALU.min)
-            nc.vector.tensor_tensor(capped[:], upper, votes[:, :, 2, slots], ALU.min)
-            nc.vector.tensor_tensor(gate[:], lower, capped[:], ALU.max)
+        capped = sb.tile([P, PACK, J], F32, name="capped")
+        gate = sb.tile([P, PACK, J], F32, name="gate")
+        hid = sb.tile([P, J, PACK], BF16, name="hid", align_bytes=64)
+        hid_codes = sb.tile([P, J], U32, name="hid_codes", align_bytes=64)
+        hid_plane = sb.tile([P, J], U8, name="hid_plane", align_bytes=64)
 
-            hid = sb.tile([P, HALF, PACK], BF16, name="hid%d" % h, align_bytes=64)
-            nc.vector.tensor_tensor(
-                hid[:].rearrange("p (c i) t -> p c t i", i=LINE),
-                gate[:].rearrange("p t (c i) -> p c t i", i=LINE),
-                a[:].rearrange("p t (c i) -> p c t i", i=LINE),
-                ALU.mult,
+        def put(first, width):
+            last = first + width == J
+            slots = slice(first, first + width)
+            nc.vector.quantize_mx(
+                hid_codes[:, slots].bitcast(E4M3X4), hid_plane[:, slots], hid[:, slots, :].rearrange("p j t -> p (j t)")
             )
-            hid_codes = sb.tile([P, HALF], U32, name="hid_codes%d" % h, align_bytes=64)
-            hid_plane = sb.tile([P, HALF], U8, name="hid_plane%d" % h, align_bytes=64)
-            nc.vector.quantize_mx(hid_codes[:].bitcast(E4M3X4), hid_plane[:], hid[:].rearrange("p j t -> p (j t)"))
-
+            window = slice(first + width - HALF, first + width)
+            rows = sb.tile([P, N // P, width], F32, name="rows%d" % first)
+            if first == 0 or last:
+                prods = [ps.tile([P, HALF], F32, name="prod%d_%d" % (first, c))[:] for c in range(N // P)]
+            else:
+                both = ps.tile([P, N // P, HALF], F32, name="prod%d" % first)
+                prods = [both[:, c, :] for c in range(N // P)]
             for c in range(N // P):
                 features = slice(c * P, (c + 1) * P)
-                prod = ps.tile([P, HALF], F32, name="prod%d_%d" % (h, c))
                 nc.tensor.matmul_mx(
-                    prod[:],
+                    prods[c],
                     lhsT=wb_codes[:, features].bitcast(E5M2X4),
                     lhsT_scale=wb_plane[:, features],
-                    rhs=hid_codes[:].bitcast(E4M3X4),
-                    rhs_scale=hid_plane[:],
+                    rhs=hid_codes[:, window].bitcast(E4M3X4),
+                    rhs_scale=hid_plane[:, window],
                     start=True,
                     stop=True,
                 )
-                rows = sb.tile([P, HALF], F32, name="rows%d_%d" % (h, c))
-                if h == 0:
-                    nc.scalar.copy(rows[:], prod[:])
-                else:
-                    nc.vector.tensor_copy(rows[:], prod[:])
+                if first == 0 and c == 0:
+                    nc.scalar.copy(rows[:, c, :], prods[c])
+                elif first == 0 or last:
+                    nc.vector.tensor_copy(rows[:, c, :], prods[c][:, HALF - width :])
+            if first > 0 and not last:
+                nc.vector.tensor_copy(rows[:], both[:, :, HALF - width :])
+            for c in range(N // P):
                 nc.scalar.activation(
-                    pages[c][:].indirect(page_list[:, h * HALF // 16 : (h + 1) * HALF // 16]),
-                    rows[:],
+                    pages[c][:].indirect(page_list[:, first // 16 : (first + width) // 16]),
+                    rows[:, c, :],
                     COPY,
                     scale=out_weight[:, c : c + 1],
                 )
+
+        for first, width in CHUNKS:
+            slots = slice(first, first + width)
+            a = banks[first // HALF][:, :, first % HALF : first % HALF + width]
+            if first % HALF == 0:
+                half = slice(first, first + HALF)
+                one, other = late_pairs[:, :, 0, half], late_pairs[:, :, 1, half]
+                nc.vector.tensor_tensor(bounds[:, 0, EARLY:, half], one, other, ALU.max)
+                nc.vector.tensor_tensor(bounds[:, 1, EARLY:, half], one, other, ALU.min)
+            nc.vector.tensor_tensor(capped[:, :, slots], bounds[:, 0, :, slots], thirds[:, :, slots], ALU.min)
+            nc.vector.tensor_tensor(gate[:, :, slots], bounds[:, 1, :, slots], capped[:, :, slots], ALU.max)
+            nc.vector.tensor_tensor(
+                hid[:, slots, :].rearrange("p (c i) t -> p c t i", i=LINE),
+                gate[:, :, slots].rearrange("p t (c i) -> p c t i", i=LINE),
+                a.rearrange("p t (c i) -> p c t i", i=LINE),
+                ALU.mult,
+            )
+            put(first, width)
 
         for c in range(N // P):
             nc.sync.dma_start(out[c * P : (c + 1) * P, :], pages[c][:])

@@ -54,6 +54,10 @@ def tile_list_majority_kernel(tc, xt_words, xt_scales, w_words, w_scales, ca, st
         wb_plane = sb.tile([P, N], U8, name="wb_plane", align_bytes=64)
         pages = [sb.tile([P, E], F32, name="page%d" % c) for c in range(N // P)]
 
+        warm = sb.tile([P, 2], F32, name="warm")
+        nc.gpsimd.memset(warm[:, 0:1], 0.0)
+        nc.scalar.activation(warm[:, 1:2], warm[:, 0:1], COPY)
+
         for plane in (w_plane, xt_plane, wb_plane):
             nc.vector.memset(plane[:].bitcast(I32), 0)
         for page in pages:

from contextlib import ExitStack

import concourse.mybir as mybir

K, T, J, R, V, N, E = 512, 1024, 256, 512, 1024, 256, 512
FLOPS = 2 * K * R * J + 2 * R * N * J

F32 = mybir.dt.float32
BF16 = mybir.dt.bfloat16
I32 = mybir.dt.int32
U32 = mybir.dt.uint32
U16 = mybir.dt.uint16
U8 = mybir.dt.uint8
FP8 = mybir.dt.float8_e4m3fn
E4M3X4 = mybir.dt.float8_e4m3fn_x4
E5M2X4 = mybir.dt.float8_e5m2_x4
E2M1X4 = mybir.dt.float4_e2m1fn_x4
ALU = mybir.AluOpType
COPY = mybir.ActivationFunctionType.Copy
RELU = mybir.ActivationFunctionType.Relu

P = 128
PACK = 4
VOTES = 3
HALF = J // 2
LINE = 4
EARLY = 2
CHUNKS = ((0, 128), (128, 64), (192, 64))


def load_scale_rows(nc, plane, rows):
    for q in range(4):
        nc.sync.dma_start(plane[32 * q : 32 * q + 4, :].bitcast(I32), rows[4 * q : 4 * q + 4, :].bitcast(I32))


def tile_list_majority_kernel(tc, xt_words, xt_scales, w_words, w_scales, ca, st, wb_words, wb_scales, so,
                                 offs, offs2, offs3, offs4, offs5, out):
    nc = tc.nc
    with ExitStack() as ctx:
        sb = ctx.enter_context(tc.tile_pool(name="sb", bufs=1))
        ps = ctx.enter_context(tc.psum_pool(name="ps", bufs=1))

        token_list = sb.tile([P, J // 16], U16, name="token_list")
        vote_lists = [sb.tile([P, J // 16], U16, name="vote_list%d" % v) for v in range(VOTES)]
        page_list = sb.tile([P, J // 16], U16, name="page_list")
        store = [sb.tile([P, V], U8, name="store%d" % t) for t in range(PACK)]
        step = sb.tile([P, PACK], F32, name="step")
        out_weight = sb.tile([P, N // P], F32, name="out_weight")
        xt_codes = sb.tile([P, T], U32, name="xt_codes")
        xt_plane = sb.tile([P, T], U8, name="xt_plane")
        w_codes = sb.tile([P, R], U16, name="w_codes")
        w_plane = sb.tile([P, R], U8, name="w_plane")
        wb_codes = sb.tile([P, N], U32, name="wb_codes", align_bytes=64)
        wb_plane = sb.tile([P, N], U8, name="wb_plane", align_bytes=64)
        pages = [sb.tile([P, E], F32, name="page%d" % c) for c in range(N // P)]

        warm = sb.tile([P, 2], F32, name="warm")
        nc.gpsimd.memset(warm[:, 0:1], 0.0)
        nc.scalar.activation(warm[:, 1:2], warm[:, 0:1], COPY)

        for plane in (w_plane, xt_plane, wb_plane):
            nc.vector.memset(plane[:].bitcast(I32), 0)
        for page in pages:
            nc.vector.memset(page[:], 0.0)

        ca_rows = ca.rearrange("(p t) v -> t p v", t=PACK)
        nc.sync.dma_start(store[0][:], ca_rows[0])
        for tile, src in zip(vote_lists, (offs2, offs3)):
            nc.sync.dma_start(tile[:], src)
        nc.sync.dma_start(store[1][:], ca_rows[1])
        load_scale_rows(nc, w_plane, w_scales[0])
        nc.sync.dma_start(step[:], st.rearrange("(p t) o -> p (t o)", t=PACK))
        for t in range(2, PACK):
            nc.sync.dma_start(store[t][:], ca_rows[t])
        nc.sync.dma_start(xt_codes[:].bitcast(I32), xt_words[0].rearrange("p c b -> p (c b)").bitcast(I32))
        nc.sync.dma_start(token_list[:], offs)
        load_scale_rows(nc, xt_plane, xt_scales[0])
        nc.sync.dma_start(vote_lists[2][:], offs4)
        nc.sync.dma_start(w_codes[:].bitcast(I32), w_words[0].bitcast(I32))
        nc.sync.dma_start(wb_codes[:].bitcast(I32), wb_words[0].rearrange("p c b -> p (c b)").bitcast(I32))
        load_scale_rows(nc, wb_plane, wb_scales[0])
        nc.sync.dma_start(page_list[:], offs5)
        with nc.allow_non_contiguous_dma(reason="one weight a partition"):
            nc.sync.dma_start(out_weight[:], so.rearrange("(c p) o -> p (c o)", p=P))

        w_dealt_plane = sb.tile([P, PACK, P], U8, name="w_dealt_plane", align_bytes=64)

        nc.gpsimd.tensor_copy(w_dealt_plane[:], w_plane[:].rearrange("p (m t) -> p t m", t=PACK))

        bounds = sb.tile([P, 2, PACK, J], F32, name="bounds")
        picked_pairs = []
        for t in range(PACK):
            picked = sb.tile([P, 2, J], U8, name="picked_pair%d" % t)
            for v in range(2):
                nc.vector.tensor_copy(picked[:, v, :], store[t][:].indirect(vote_lists[v][:]))
            picked_pairs.append(picked[:].rearrange("p v j -> p (v j)").bitcast(FP8))
            if t < EARLY:
                pair = sb.tile([P, 2, J], F32, name="pair%d" % t)
                gap = sb.tile([P, J], F32, name="gap%d" % t, tag="gap%d" % t, align_bytes=64)
                excess = sb.tile([P, J], F32, name="excess%d" % t)
                nc.scalar.activation(
                    pair[:].rearrange("p v j -> p (v j)"), picked_pairs[t], COPY, scale=step[:, t : t + 1]
                )
                nc.gpsimd.tensor_tensor(gap[:], pair[:, 0, :], pair[:, 1, :], ALU.subtract)
                nc.scalar.activation(excess[:], gap[:], RELU)
                nc.gpsimd.tensor_tensor(bounds[:, 0, t, :], pair[:, 1, :], excess[:], ALU.add)
                nc.gpsimd.tensor_tensor(bounds[:, 1, t, :], pair[:, 0, :], excess[:], ALU.subtract)

        x_codes = sb.tile([P, J], U32, name="x_codes", align_bytes=64)
        x_plane = sb.tile([P, J], U8, name="x_plane", align_bytes=64)
        nc.vector.tensor_copy(x_codes[:], xt_codes[:].indirect(token_list[:]))
        nc.vector.tensor_copy(x_plane[:], xt_plane[:].indirect(token_list[:]))

        rest = sb.tile([P, PACK + 2 * (PACK - EARLY), J], F32, name="rest", tag="gap%d" % (EARLY - 1), align_bytes=64)
        thirds = rest[:, :PACK, :]
        late_pairs = rest[:, PACK:, :].rearrange("p (t v) j -> p t v j", v=2)
        for t in range(EARLY, PACK):
            nc.scalar.activation(
                late_pairs[:, t - EARLY, :, :].rearrange("p v j -> p (v j)"),
                picked_pairs[t],
                COPY,
                scale=step[:, t : t + 1],
            )
        for t in range(PACK):
            picked = sb.tile([P, J], U8, name="picked_third%d" % t)
            nc.vector.tensor_copy(picked[:], store[t][:].indirect(vote_lists[2][:]))
            nc.scalar.activation(thirds[:, t, :], picked[:].bitcast(FP8), COPY, scale=step[:, t : t + 1])

        w_dealt = sb.tile([P, PACK, P], U16, name="w_dealt", tag="gap0", align_bytes=64)
        nc.scalar.copy(w_dealt[:], w_codes[:].rearrange("p (m t) -> p t m", t=PACK))

        banks = []
        for h in range(J // HALF):
            slots = slice(h * HALF, (h + 1) * HALF)
            a = ps.tile([P, PACK, HALF], F32, name="a%d" % h)
            for t in range(PACK):
                nc.tensor.matmul_mx(
                    a[:, t, :],
                    lhsT=w_dealt[:, t, :].bitcast(E2M1X4),
                    lhsT_scale=w_dealt_plane[:, t, :],
                    rhs=x_codes[:, slots].bitcast(E4M3X4),
                    rhs_scale=x_plane[:, slots],
                    start=True,
                    stop=True,
                )
            banks.append(a)

        capped = sb.tile([P, PACK, J], F32, name="capped")
        gate = sb.tile([P, PACK, J], F32, name="gate")
        hid = sb.tile([P, J, PACK], BF16, name="hid", align_bytes=64)
        hid_codes = sb.tile([P, J], U32, name="hid_codes", align_bytes=64)
        hid_plane = sb.tile([P, J], U8, name="hid_plane", align_bytes=64)

        def put(first, width):
            last = first + width == J
            slots = slice(first, first + width)
            nc.vector.quantize_mx(
                hid_codes[:, slots].bitcast(E4M3X4), hid_plane[:, slots], hid[:, slots, :].rearrange("p j t -> p (j t)")
            )
            window = slice(first + width - HALF, first + width)
            rows = sb.tile([P, N // P, width], F32, name="rows%d" % first)
            if first == 0 or last:
                prods = [ps.tile([P, HALF], F32, name="prod%d_%d" % (first, c))[:] for c in range(N // P)]
            else:
                both = ps.tile([P, N // P, HALF], F32, name="prod%d" % first)
                prods = [both[:, c, :] for c in range(N // P)]
            for c in range(N // P):
                features = slice(c * P, (c + 1) * P)
                nc.tensor.matmul_mx(
                    prods[c],
                    lhsT=wb_codes[:, features].bitcast(E5M2X4),
                    lhsT_scale=wb_plane[:, features],
                    rhs=hid_codes[:, window].bitcast(E4M3X4),
                    rhs_scale=hid_plane[:, window],
                    start=True,
                    stop=True,
                )
                if first == 0 and c == 0:
                    nc.scalar.copy(rows[:, c, :], prods[c])
                elif first == 0 or last:
                    nc.vector.tensor_copy(rows[:, c, :], prods[c][:, HALF - width :])
            if first > 0 and not last:
                nc.vector.tensor_copy(rows[:], both[:, :, HALF - width :])
            for c in range(N // P):
                nc.scalar.activation(
                    pages[c][:].indirect(page_list[:, first // 16 : (first + width) // 16]),
                    rows[:, c, :],
                    COPY,
                    scale=out_weight[:, c : c + 1],
                )

        for first, width in CHUNKS:
            slots = slice(first, first + width)
            a = banks[first // HALF][:, :, first % HALF : first % HALF + width]
            if first % HALF == 0:
                half = slice(first, first + HALF)
                one, other = late_pairs[:, :, 0, half], late_pairs[:, :, 1, half]
                nc.vector.tensor_tensor(bounds[:, 0, EARLY:, half], one, other, ALU.max)
                nc.vector.tensor_tensor(bounds[:, 1, EARLY:, half], one, other, ALU.min)
            nc.vector.tensor_tensor(capped[:, :, slots], bounds[:, 0, :, slots], thirds[:, :, slots], ALU.min)
            nc.vector.tensor_tensor(gate[:, :, slots], bounds[:, 1, :, slots], capped[:, :, slots], ALU.max)
            nc.vector.tensor_tensor(
                hid[:, slots, :].rearrange("p (c i) t -> p c t i", i=LINE),
                gate[:, :, slots].rearrange("p t (c i) -> p c t i", i=LINE),
                a.rearrange("p t (c i) -> p c t i", i=LINE),
                ALU.mult,
            )
            put(first, width)

        for c in range(N // P):
            nc.sync.dma_start(out[c * P : (c + 1) * P, :], pages[c][:])
